import numpy as np
import ml_dtypes


def mxq(x, axis, fmt="e4m3"):
    dtype, down = {"e4m3": (ml_dtypes.float8_e4m3fn, 7), "e5m2": (ml_dtypes.float8_e5m2, 14)}[fmt]
    v = np.moveaxis(np.asarray(x, np.float32).astype(ml_dtypes.bfloat16).astype(np.float64), axis, -1)
    blocks = v.reshape(v.shape[:-1] + (-1, 32))
    amax = np.abs(blocks).max(-1, keepdims=True)
    byte = np.maximum(np.where(amax > 0, np.frexp(amax)[1] - 1 + 127, 0) - down, 1)
    scale = np.exp2(byte - 127.0)
    codes = (blocks / scale).astype(np.float32).astype(dtype).astype(np.float64)
    return np.moveaxis((codes * scale).reshape(v.shape), -1, axis)


WIDE = False


def mx_kscale(k):
    if not WIDE:
        return np.ones(k)
    levels = np.array([10, -10, 5, -5, 0])
    if k % 512:
        return np.exp2(np.random.permutation(np.resize(levels, k // 32))).repeat(32)
    a = np.empty((k // 512, 16))
    for p in range(k // 512):
        a[p, :8] = np.random.permutation(np.resize(levels, 8))
        for g in range(8):
            far = levels[np.abs(levels - a[p, g]) >= 10]
            a[p, g + 8] = far[np.random.randint(len(far))]
    return np.exp2(a.ravel()).repeat(32)


def f64(x):
    return np.asarray(x).astype(np.float64)


def striped(idx):
    return np.tile(idx.reshape(-1, 16).T, (8, 1)).astype(np.uint16)


def unstriped(offs):
    return offs[:16].T.reshape(-1).astype(np.int64)


E2M1 = np.array([0.0, 0.5, 1.0, 1.5, 2.0, 3.0, 4.0, 6.0, -0.0, -0.5, -1.0, -1.5, -2.0, -3.0, -4.0, -6.0])


def pack_weight(w, fmt):
    k, n = w.shape
    w = f64(np.asarray(w, np.float32).astype(ml_dtypes.bfloat16)).reshape(k // 32, 32, n)
    amax = np.abs(w).max(1)
    if fmt == "e4m3":
        byte = np.frexp(amax)[1] - 1 + 127 - 7
    else:
        mant, ex = np.frexp(amax / 6.0)
        byte = np.where(mant > 0.5, ex, ex - 1) + 127
    byte = np.clip(np.where(amax > 0, byte, 1), 1, 254)
    scaled = (w * np.exp2(127.0 - byte)[:, None, :]).reshape(k, n).astype(np.float32)
    by_word = np.ascontiguousarray(scaled.reshape(k // 512, 128, 4, n).transpose(0, 1, 3, 2))
    if fmt == "e4m3":
        words = by_word.astype(ml_dtypes.float8_e4m3fn).view(np.uint8)
    else:
        c = by_word.astype(ml_dtypes.float4_e2m1fn).view(np.uint8) & 0xF
        words = (c[..., 0::2] | (c[..., 1::2] << 4)).reshape(k // 512, 128, 2 * n)
    return np.ascontiguousarray(words), np.ascontiguousarray(byte.astype(np.uint8).reshape(k // 512, 16, n))


def unpack_weight(words, scales, fmt):
    g, _, n = scales.shape
    words = np.ascontiguousarray(words).reshape(g, 128, n, -1)
    if fmt == "e4m3":
        vals = words.view(ml_dtypes.float8_e4m3fn).astype(np.float64)
    else:
        nib = np.empty((g, 128, n, 4), np.uint8)
        nib[..., 0::2] = words & 0xF
        nib[..., 1::2] = words >> 4
        vals = E2M1[nib]
    vals = vals * np.repeat(np.exp2(scales.astype(np.float64) - 127.0), 8, axis=1)[..., None]
    return vals.transpose(0, 1, 3, 2).reshape(g * 512, n)


def gelu(v):
    return 0.5 * v * (1.0 + np.tanh(np.sqrt(2.0 / np.pi) * (v + 0.044715 * v**3)))


K, T, S, H, N, K2, T2, P = 1024, 4096, 1024, 512, 512, 512, 2048, 512


def setup_inputs():
    n = np.random.standard_normal
    s = mx_kscale(K)[:, None]
    s2 = mx_kscale(K2)[:, None]
    u = mx_kscale(H)[:, None]
    tab_words, tab_scales = pack_weight(n((K, T)) * s, "e4m3")
    tab2_words, tab2_scales = pack_weight(n((K2, T2)) * s2, "e4m3")
    w1_words, w1_scales = pack_weight(1.2 * n((K, H)) / np.sqrt(K) / s, "e2m1")
    w4_words, w4_scales = pack_weight(1.2 * n((H, N)) / np.sqrt(H) / u, "e4m3")
    return {
        "tab_words": tab_words, "tab_scales": tab_scales,
        "offs": striped(np.random.permutation(T)[:S]),
        "tab2_words": tab2_words, "tab2_scales": tab2_scales,
        "offs2": striped(np.random.permutation(T2)[:P]),
        "pos1": striped(np.random.permutation(S)[:P]),
        "w1_words": w1_words, "w1_scales": w1_scales,
        "b1": (0.5 * n(H)).astype(np.float32),
        "w2": (0.5 * n((K, H)) / np.sqrt(K) / s).astype(np.float32),
        "gain": (np.exp(0.3 * n(H)) * u[:, 0]).astype(np.float32),
        "w3": (0.6 * n((K, H)) / np.sqrt(K) / s * u.T).astype(np.float32),
        "w4_words": w4_words, "w4_scales": w4_scales,
        "w5": (n((K2, N)) / np.sqrt(K2) / s2).astype(np.float32),
    }


def reference(tab_words, tab_scales, offs, tab2_words, tab2_scales, offs2, pos1,
              w1_words, w1_scales, b1, w2, gain, w3, w4_words, w4_scales, w5):
    v = unpack_weight(tab_words, tab_scales, "e4m3")[:, unstriped(offs)]
    v2 = unpack_weight(tab2_words, tab2_scales, "e4m3")[:, unstriped(offs2)]
    w1 = unpack_weight(w1_words, w1_scales, "e2m1")
    w4 = unpack_weight(w4_words, w4_scales, "e4m3")
    a = np.tanh((w1.T @ v) + f64(b1)[:, None])
    ripple = np.cos(mxq(f64(w2), 0, "e4m3").T @ v)
    direct = mxq(f64(w3), 0, "e4m3").T @ v
    h = f64(gain)[:, None] * (a * ripple) + direct
    y = w4.T @ mxq(h, 0, "e4m3")
    b = mxq(f64(w5), 0, "e4m3").T @ v2
    return np.maximum(y[:, unstriped(pos1)], b)

@@ -1,0 +1,289 @@
+from contextlib import ExitStack
+
+import concourse.mybir as mybir
+
+K, T, S, H, N, K2, T2, PAIRS = 1024, 4096, 1024, 512, 512, 512, 2048, 512
+FLOPS = 2 * (3 * K * H * S + H * N * S + K2 * N * PAIRS)
+
+F32 = mybir.dt.float32
+BF16 = mybir.dt.bfloat16
+I32 = mybir.dt.int32
+U32 = mybir.dt.uint32
+U16 = mybir.dt.uint16
+U8 = mybir.dt.uint8
+FP8X4 = mybir.dt.float8_e4m3fn_x4
+FP4X4 = mybir.dt.float4_e2m1fn_x4
+ACT = mybir.ActivationFunctionType
+ALU = mybir.AluOpType
+
+P = 128
+PACK = 4
+K_PASS = P * PACK
+PASSES = K // K_PASS
+HALF = 512
+HALVES = S // HALF
+CHUNK = 128
+CHUNKS = HALF // CHUNK
+QUADS = 4
+
+
+def tile_list_chest_cough_features_kernel(
+    tc, tab_words, tab_scales, offs, tab2_words, tab2_scales, offs2, pos1,
+    w1_words, w1_scales, b1, w2, gain, w3, w4_words, w4_scales, w5, out,
+):
+    nc = tc.nc
+    with ExitStack() as ctx:
+        keep = ctx.enter_context(tc.tile_pool(name="keep", bufs=1))
+        ring = ctx.enter_context(tc.tile_pool(name="ring", bufs=2))
+        psum = ctx.enter_context(tc.psum_pool(name="psum", bufs=1))
+
+        def held(name, shape, dtype):
+            return keep.tile(shape, dtype, name=name, align_bytes=64)
+
+        def bank(i):
+            return psum.tile([P, 512], F32, name="bank%d" % i, tag="bank%d" % i)
+
+        idx = held("idx", [P, S // 16], U16)
+        idx2 = held("idx2", [P, PAIRS // 16], U16)
+        pair = held("pair", [P, PAIRS // 16], U16)
+        tab_w = [held("tab_w%d" % a, [P, T], U32) for a in range(PASSES)]
+        tab_s = held("tab_s", [P, T], U8)
+        tab2_w = held("tab2_w", [P, T2], U32)
+        tab2_s = held("tab2_s", [P, T2], U8)
+        v_w = [[held("v_w%d_%d" % (a, h), [P, HALF], U32) for h in range(HALVES)] for a in range(PASSES)]
+        v_rows = held("v_rows", [P, S], U8)
+        v_s = held("v_s", [P, PASSES * S], U8)
+        v2_w = held("v2_w", [P, PAIRS], U32)
+        v2_rows = held("v2_rows", [P, PAIRS], U8)
+        v2_s = held("v2_s", [P, PAIRS], U8)
+        w1_raw = held("w1_raw", [P, PASSES * 2 * H], U8)
+        w1_raw_s = held("w1_raw_s", [P, PASSES * H], U8)
+        w1_w = held("w1_w", [P, PASSES * 2 * H], U8)
+        w1_s = held("w1_s", [P, PASSES * H], U8)
+        w4_w = held("w4_w", [P, N], U32)
+        w4_s = held("w4_s", [P, N], U8)
+        bias = held("bias", [P, PACK], F32)
+        gains = held("gains", [P, PACK], F32)
+        w2_raw = [held("w2_raw%d" % a, [P, PACK, H], F32) for a in range(PASSES)]
+        w3_raw = [held("w3_raw%d" % a, [P, PACK, H], F32) for a in range(PASSES)]
+        w5_raw = held("w5_raw", [P, PACK, N], F32)
+
+        nc.vector.memset(tab_s[:].bitcast(I32), 0)
+        nc.vector.memset(tab2_s[:].bitcast(I32), 0)
+        nc.gpsimd.memset(w1_raw_s[:].bitcast(I32), 0)
+        nc.gpsimd.memset(v_s[:].bitcast(I32), 0)
+        nc.gpsimd.memset(v2_s[:].bitcast(I32), 0)
+        nc.gpsimd.memset(w4_s[:].bitcast(I32), 0)
+
+        def load_words(dst, src, c0, c1):
+            flat = src.rearrange("p n t -> p (n t)")
+            nc.sync.dma_start(dst[:, c0:c1].bitcast(I32), flat[:, PACK * c0 : PACK * c1].bitcast(I32))
+
+        def load_weight(dst, src, a):
+            rows = src[a * K_PASS : (a + 1) * K_PASS, :]
+            nc.sync.dma_start(dst[:], rows.rearrange("(p j) c -> p j c", j=PACK))
+
+        nc.sync.dma_start(idx[:], offs)
+        load_words(tab_w[0], tab_words[0], 0, T // 2)
+        nc.scalar.dma_start(tab_s[0:P:4, :].bitcast(I32), tab_scales.bitcast(I32).rearrange("a q c -> q a c"))
+        nc.sync.dma_start(idx2[:], offs2)
+        nc.scalar.dma_start(tab2_s[0:P:8, :].bitcast(I32), tab2_scales[0].bitcast(I32))
+        load_words(tab_w[0], tab_words[0], T // 2, T)
+        nc.sync.dma_start(
+            w1_raw[:].bitcast(I32).rearrange("p (a c) -> p a c", a=PASSES),
+            w1_words.bitcast(I32).rearrange("a p c -> p a c"),
+        )
+        load_words(tab_w[1], tab_words[1], 0, T // 2)
+        for q in range(QUADS):
+            nc.sync.dma_start(
+                w1_raw_s[32 * q : 32 * q + 4, :].bitcast(I32).rearrange("r (a c) -> r a c", a=PASSES),
+                w1_scales.bitcast(I32)[:, 4 * q : 4 * q + 4, :].rearrange("a r c -> r a c"),
+            )
+        nc.sync.dma_start(bias[:], b1.rearrange("(p t) -> p t", t=PACK))
+        nc.sync.dma_start(gains[:], gain.rearrange("(p t) -> p t", t=PACK))
+        load_words(tab_w[1], tab_words[1], T // 2, T)
+        load_weight(w2_raw[0], w2, 0)
+
+        nc.vector.tensor_copy(v_rows[:], tab_s[:].indirect(idx[:]))
+        for q in range(QUADS):
+            nc.scalar.dma_start(
+                v_s[32 * q : 32 * q + 4, :].bitcast(I32).rearrange("r (a c) -> r a c", a=PASSES),
+                v_rows[32 * q : 32 * q + 32 : 4, :].bitcast(I32),
+            )
+
+        load_weight(w2_raw[1], w2, 1)
+        load_weight(w3_raw[0], w3, 0)
+        load_weight(w3_raw[1], w3, 1)
+        load_words(w4_w, w4_words[0], 0, N)
+        for q in range(QUADS):
+            nc.sync.dma_start(w4_s[32 * q : 32 * q + 4, :].bitcast(I32), w4_scales[0].bitcast(I32)[4 * q : 4 * q + 4, :])
+        load_weight(w5_raw, w5, 0)
+        nc.sync.dma_start(pair[:], pos1)
+        load_words(tab2_w, tab2_words[0], 0, T2)
+
+        def gather_words(a, h):
+            cols = slice(h * HALF // 16, (h + 1) * HALF // 16)
+            nc.vector.tensor_copy(v_w[a][h][:], tab_w[a][:].indirect(idx[:, cols]))
+
+        for h in range(HALVES):
+            gather_words(0, h)
+        nc.vector.tensor_copy(v2_rows[:], tab2_s[:].indirect(idx2[:]))
+        for q in range(QUADS):
+            nc.sync.dma_start(v2_s[32 * q : 32 * q + 4, :].bitcast(I32), v2_rows[32 * q : 32 * q + 32 : 8, :].bitcast(I32))
+
+        nc.vector.tensor_copy(
+            w1_w[:].bitcast(U16).rearrange("p (a t m) -> p a t m", a=PASSES, t=PACK),
+            w1_raw[:].bitcast(U16).rearrange("p (a m t) -> p a t m", a=PASSES, t=PACK),
+        )
+        nc.vector.tensor_copy(
+            w1_s[:].rearrange("p (a t m) -> p a t m", a=PASSES, t=PACK),
+            w1_raw_s[:].rearrange("p (a m t) -> p a t m", a=PASSES, t=PACK),
+        )
+
+        two_abs = held("two_abs", [P, PACK], F32)
+        abs_gain = held("abs_gain", [P, PACK], F32)
+        flip = held("flip", [P, PACK], F32)
+        flip_bias = held("flip_bias", [P, PACK], F32)
+        halves = held("halves", [P, PACK], F32)
+        root = held("root", [P, PACK], F32)
+        nc.scalar.activation(two_abs[:], gains[:], ACT.Abs, scale=2.0)
+        nc.scalar.activation(abs_gain[:], gains[:], ACT.Abs)
+        nc.scalar.activation(flip[:], gains[:], ACT.Sign, scale=-1.0)
+        nc.gpsimd.memset(halves[:], 0.5)
+        nc.gpsimd.tensor_tensor(root[:], two_abs[:], halves[:], ALU.pow)
+        nc.gpsimd.tensor_tensor(flip_bias[:], bias[:], flip[:], ALU.mult)
+
+        for h in range(HALVES):
+            gather_words(1, h)
+
+        def v_scale(a, c0, width):
+            return v_s[:, a * S + c0 : a * S + c0 + width]
+
+        mix = [held("mix%d" % h, [P, PACK, HALF], F32) for h in range(HALVES)]
+        z1 = [[bank(PACK * h + t) for t in range(PACK)] for h in range(HALVES)]
+        for a in range(PASSES):
+            for h in range(HALVES):
+                for t in range(PACK):
+                    c = a * H + t * P
+                    nc.tensor.matmul_mx(
+                        z1[h][t][:],
+                        lhsT=w1_w[:, 2 * c : 2 * (c + P)].bitcast(FP4X4), lhsT_scale=w1_s[:, c : c + P],
+                        rhs=v_w[a][h][:].bitcast(FP8X4), rhs_scale=v_scale(a, h * HALF, HALF),
+                        start=(a == 0), stop=(a == PASSES - 1),
+                    )
+        for h in range(HALVES):
+            for t in range(PACK):
+                nc.scalar.activation(
+                    mix[h][:, t, :], z1[h][t][:], ACT.Tanh, bias=flip_bias[:, t : t + 1], scale=flip[:, t : t + 1]
+                )
+
+        def quantised(name, raw, dealt):
+            rounded = ring.tile([P, PACK * 512], BF16, name="rounded", align_bytes=64)
+            if dealt:
+                nc.vector.tensor_copy(
+                    rounded[:].rearrange("p (t m j) -> p m t j", t=PACK, j=PACK),
+                    raw[:].rearrange("p j (m t) -> p m t j", t=PACK),
+                )
+            else:
+                nc.scalar.copy(
+                    rounded[:].rearrange("p (c i j) -> p c j i", i=PACK, j=PACK),
+                    raw[:].rearrange("p j (c i) -> p c j i", i=PACK),
+                )
+            return rounded
+
+        def quantise(name, rounded):
+            codes = held(name + "_w", [P, 512], U32)
+            scales = held(name + "_s", [P, 512], U8)
+            nc.vector.quantize_mx(out=codes[:].bitcast(FP8X4), scales=scales[:], in_=rounded[:])
+            return codes, scales
+
+        w2_q = [quantise("w2_%d" % a, quantised("w2", w2_raw[a], True)) for a in range(PASSES)]
+        w3_q = [quantise("w3_%d" % a, quantised("w3", w3_raw[a], True)) for a in range(PASSES)]
+
+        y_rows = [held("y_rows%d" % n, [P, S], F32) for n in range(N // P)]
+
+        waves = {}
+
+        def sine(h, t):
+            z2 = bank(PACK * h + t)
+            for a in range(PASSES):
+                codes, scales = w2_q[a]
+                nc.tensor.matmul_mx(
+                    z2[:],
+                    lhsT=codes[:, t * P : (t + 1) * P].bitcast(FP8X4), lhsT_scale=scales[:, t * P : (t + 1) * P],
+                    rhs=v_w[a][h][:].bitcast(FP8X4), rhs_scale=v_scale(a, h * HALF, HALF),
+                    start=(a == 0), stop=(a == PASSES - 1),
+                )
+            wave = ring.tile([P, HALF], F32, name="wave", bufs=4)
+            nc.scalar.activation(wave[:], z2[:], ACT.Sin, scale=0.5)
+            waves[h, t] = wave
+
+        def ripple(h, t):
+            wave = waves[h, t]
+            nc.scalar.activation(wave[:], wave[:], ACT.Square, scale=root[:, t : t + 1])
+            nc.vector.scalar_tensor_tensor(
+                mix[h][:, t, :], wave[:], abs_gain[:, t : t + 1], mix[h][:, t, :], ALU.subtract, ALU.mult
+            )
+
+        h_round = [held("h_round%d" % h, [P, PACK * HALF], BF16) for h in range(HALVES)]
+
+        def reading(h, c):
+            z3 = bank((CHUNKS * h + c) % 3)
+            cols = slice(c * CHUNK, (c + 1) * CHUNK)
+            for t in range(PACK):
+                for a in range(PASSES):
+                    codes, scales = w3_q[a]
+                    nc.tensor.matmul_mx(
+                        z3[:, t * CHUNK : (t + 1) * CHUNK],
+                        lhsT=codes[:, t * P : (t + 1) * P].bitcast(FP8X4), lhsT_scale=scales[:, t * P : (t + 1) * P],
+                        rhs=v_w[a][h][:, cols].bitcast(FP8X4), rhs_scale=v_scale(a, h * HALF + c * CHUNK, CHUNK),
+                        start=(a == 0), stop=(a == PASSES - 1),
+                    )
+            nc.vector.tensor_tensor(
+                h_round[h][:, PACK * c * CHUNK : PACK * (c + 1) * CHUNK].rearrange("p (c i t) -> p c t i", i=PACK, t=PACK),
+                z3[:].rearrange("p (t c i) -> p c t i", t=PACK, i=PACK),
+                mix[h][:, :, cols].rearrange("p t (c i) -> p c t i", i=PACK),
+                ALU.add,
+            )
+
+        def features(h, banks):
+            codes, scales = quantise("h_%d" % h, h_round[h])
+            for n in range(N // P):
+                y = bank(banks[n])
+                nc.tensor.matmul_mx(
+                    y[:],
+                    lhsT=w4_w[:, n * P : (n + 1) * P].bitcast(FP8X4), lhsT_scale=w4_s[:, n * P : (n + 1) * P],
+                    rhs=codes[:].bitcast(FP8X4), rhs_scale=scales[:],
+                    start=True, stop=True,
+                )
+                nc.scalar.copy(y_rows[n][:, h * HALF : (h + 1) * HALF], y[:])
+
+        steps = [(h, t) for h in range(HALVES) for t in range(PACK)]
+        sine(*steps[0])
+        for i, (h, t) in enumerate(steps):
+            if i + 1 < len(steps):
+                sine(*steps[i + 1])
+            if h == 1:
+                reading(0, t)
+            ripple(h, t)
+        features(0, (3, 4, 5, 6))
+        w5_round = quantised("w5", w5_raw, False)
+        for c in range(CHUNKS):
+            reading(1, c)
+        features(1, (0, 1, 2, 3))
+
+        nc.vector.tensor_copy(v2_w[:], tab2_w[:].indirect(idx2[:]))
+        w5_codes, w5_scales = quantise("w5", w5_round)
+        for n in range(N // P):
+            b = bank(4 + n)
+            nc.tensor.matmul_mx(
+                b[:],
+                lhsT=w5_codes[:, n * P : (n + 1) * P].bitcast(FP8X4), lhsT_scale=w5_scales[:, n * P : (n + 1) * P],
+                rhs=v2_w[:].bitcast(FP8X4), rhs_scale=v2_s[:],
+                start=True, stop=True,
+            )
+            picked = ring.tile([P, PAIRS], F32, name="picked")
+            nc.vector.tensor_copy(picked[:], y_rows[n][:].indirect(pair[:]))
+            result = ring.tile([P, PAIRS], F32, name="result", bufs=4)
+            nc.vector.tensor_tensor(result[:], b[:], picked[:], ALU.max)
+            nc.sync.dma_start(out[n * P : (n + 1) * P, :], result[:])

@@ -37,8 +37,8 @@ def tile_list_chest_cough_features_kernel(
         ring = ctx.enter_context(tc.tile_pool(name="ring", bufs=2))
         psum = ctx.enter_context(tc.psum_pool(name="psum", bufs=1))
 
-        def held(name, shape, dtype):
-            return keep.tile(shape, dtype, name=name, align_bytes=64)
+        def held(name, shape, dtype, tag=None):
+            return keep.tile(shape, dtype, name=name, tag=tag or name, align_bytes=64)
 
         def bank(i):
             return psum.tile([P, 512], F32, name="bank%d" % i, tag="bank%d" % i)
@@ -53,7 +53,6 @@ def tile_list_chest_cough_features_kernel(
         v_w = [[held("v_w%d_%d" % (a, h), [P, HALF], U32) for h in range(HALVES)] for a in range(PASSES)]
         v_rows = held("v_rows", [P, S], U8)
         v_s = held("v_s", [P, PASSES * S], U8)
-        v2_w = held("v2_w", [P, PAIRS], U32)
         v2_rows = held("v2_rows", [P, PAIRS], U8)
         v2_s = held("v2_s", [P, PAIRS], U8)
         w1_raw = held("w1_raw", [P, PASSES * 2 * H], U8)
@@ -68,12 +67,12 @@ def tile_list_chest_cough_features_kernel(
         w3_raw = [held("w3_raw%d" % a, [P, PACK, H], F32) for a in range(PASSES)]
         w5_raw = held("w5_raw", [P, PACK, N], F32)
 
-        nc.vector.memset(tab_s[:].bitcast(I32), 0)
-        nc.vector.memset(tab2_s[:].bitcast(I32), 0)
         nc.gpsimd.memset(w1_raw_s[:].bitcast(I32), 0)
-        nc.gpsimd.memset(v_s[:].bitcast(I32), 0)
-        nc.gpsimd.memset(v2_s[:].bitcast(I32), 0)
-        nc.gpsimd.memset(w4_s[:].bitcast(I32), 0)
+        nc.vector.memset(tab_s[32:64, :].bitcast(I32), 0)
+        nc.vector.memset(tab_s[64:P, :].bitcast(I32), 0)
+
+        for plane in (v_s, tab2_s, v2_s, w4_s):
+            nc.vector.memset(plane[:].bitcast(I32), 0)
 
         def load_words(dst, src, c0, c1):
             flat = src.rearrange("p n t -> p (n t)")
@@ -84,54 +83,48 @@ def tile_list_chest_cough_features_kernel(
             nc.sync.dma_start(dst[:], rows.rearrange("(p j) c -> p j c", j=PACK))
 
         nc.sync.dma_start(idx[:], offs)
-        load_words(tab_w[0], tab_words[0], 0, T // 2)
-        nc.scalar.dma_start(tab_s[0:P:4, :].bitcast(I32), tab_scales.bitcast(I32).rearrange("a q c -> q a c"))
-        nc.sync.dma_start(idx2[:], offs2)
-        nc.scalar.dma_start(tab2_s[0:P:8, :].bitcast(I32), tab2_scales[0].bitcast(I32))
-        load_words(tab_w[0], tab_words[0], T // 2, T)
-        nc.sync.dma_start(
+        nc.scalar.dma_start(tab_s[0:32, :].bitcast(I32), tab_scales.bitcast(I32).rearrange("a q c -> q a c"))
+        nc.scalar.dma_start(
             w1_raw[:].bitcast(I32).rearrange("p (a c) -> p a c", a=PASSES),
             w1_words.bitcast(I32).rearrange("a p c -> p a c"),
         )
-        load_words(tab_w[1], tab_words[1], 0, T // 2)
         for q in range(QUADS):
-            nc.sync.dma_start(
+            nc.gpsimd.dma_start(
                 w1_raw_s[32 * q : 32 * q + 4, :].bitcast(I32).rearrange("r (a c) -> r a c", a=PASSES),
                 w1_scales.bitcast(I32)[:, 4 * q : 4 * q + 4, :].rearrange("a r c -> r a c"),
             )
-        nc.sync.dma_start(bias[:], b1.rearrange("(p t) -> p t", t=PACK))
-        nc.sync.dma_start(gains[:], gain.rearrange("(p t) -> p t", t=PACK))
+        nc.gpsimd.dma_start(gains[:], gain.rearrange("(p t) -> p t", t=PACK))
+        nc.gpsimd.dma_start(bias[:], b1.rearrange("(p t) -> p t", t=PACK))
+        nc.gpsimd.dma_start(tab2_s[0:P:8, :].bitcast(I32), tab2_scales[0].bitcast(I32))
+        load_words(tab_w[0], tab_words[0], 0, T // 2)
+        load_words(tab_w[0], tab_words[0], T // 2, T)
+        nc.sync.dma_start(idx2[:], offs2)
+        load_words(tab_w[1], tab_words[1], 0, T // 2)
         load_words(tab_w[1], tab_words[1], T // 2, T)
         load_weight(w2_raw[0], w2, 0)
+        load_weight(w2_raw[1], w2, 1)
+        load_weight(w3_raw[0], w3, 0)
+        load_weight(w3_raw[1], w3, 1)
+        nc.sync.dma_start(pair[:], pos1)
+        load_words(w4_w, w4_words[0], 0, N)
+        load_weight(w5_raw, w5, 0)
+        load_words(tab2_w, tab2_words[0], 0, T2)
+        for q in range(QUADS):
+            nc.sync.dma_start(w4_s[32 * q : 32 * q + 4, :].bitcast(I32), w4_scales[0].bitcast(I32)[4 * q : 4 * q + 4, :])
 
         nc.vector.tensor_copy(v_rows[:], tab_s[:].indirect(idx[:]))
         for q in range(QUADS):
             nc.scalar.dma_start(
                 v_s[32 * q : 32 * q + 4, :].bitcast(I32).rearrange("r (a c) -> r a c", a=PASSES),
-                v_rows[32 * q : 32 * q + 32 : 4, :].bitcast(I32),
+                v_rows[8 * q : 8 * q + 8, :].bitcast(I32),
             )
-
-        load_weight(w2_raw[1], w2, 1)
-        load_weight(w3_raw[0], w3, 0)
-        load_weight(w3_raw[1], w3, 1)
-        load_words(w4_w, w4_words[0], 0, N)
-        for q in range(QUADS):
-            nc.sync.dma_start(w4_s[32 * q : 32 * q + 4, :].bitcast(I32), w4_scales[0].bitcast(I32)[4 * q : 4 * q + 4, :])
-        load_weight(w5_raw, w5, 0)
-        nc.sync.dma_start(pair[:], pos1)
-        load_words(tab2_w, tab2_words[0], 0, T2)
 
         def gather_words(a, h):
             cols = slice(h * HALF // 16, (h + 1) * HALF // 16)
             nc.vector.tensor_copy(v_w[a][h][:], tab_w[a][:].indirect(idx[:, cols]))
 
-        for h in range(HALVES):
-            gather_words(0, h)
-        nc.vector.tensor_copy(v2_rows[:], tab2_s[:].indirect(idx2[:]))
-        for q in range(QUADS):
-            nc.sync.dma_start(v2_s[32 * q : 32 * q + 4, :].bitcast(I32), v2_rows[32 * q : 32 * q + 32 : 8, :].bitcast(I32))
 
-        nc.vector.tensor_copy(
+        nc.scalar.copy(
             w1_w[:].bitcast(U16).rearrange("p (a t m) -> p a t m", a=PASSES, t=PACK),
             w1_raw[:].bitcast(U16).rearrange("p (a m t) -> p a t m", a=PASSES, t=PACK),
         )
@@ -139,6 +132,12 @@ def tile_list_chest_cough_features_kernel(
             w1_s[:].rearrange("p (a t m) -> p a t m", a=PASSES, t=PACK),
             w1_raw_s[:].rearrange("p (a m t) -> p a t m", a=PASSES, t=PACK),
         )
+
+        for h in range(HALVES):
+            gather_words(0, h)
+        nc.vector.tensor_copy(v2_rows[:], tab2_s[:].indirect(idx2[:]))
+        for q in range(QUADS):
+            nc.sync.dma_start(v2_s[32 * q : 32 * q + 4, :].bitcast(I32), v2_rows[32 * q : 32 * q + 32 : 8, :].bitcast(I32))
 
         two_abs = held("two_abs", [P, PACK], F32)
         abs_gain = held("abs_gain", [P, PACK], F32)
@@ -161,8 +160,8 @@ def tile_list_chest_cough_features_kernel(
 
         mix = [held("mix%d" % h, [P, PACK, HALF], F32) for h in range(HALVES)]
         z1 = [[bank(PACK * h + t) for t in range(PACK)] for h in range(HALVES)]
-        for a in range(PASSES):
-            for h in range(HALVES):
+        for h in range(HALVES):
+            for a in range(PASSES):
                 for t in range(PACK):
                     c = a * H + t * P
                     nc.tensor.matmul_mx(
@@ -191,8 +190,8 @@ def tile_list_chest_cough_features_kernel(
                 )
             return rounded
 
-        def quantise(name, rounded):
-            codes = held(name + "_w", [P, 512], U32)
+        def quantise(name, rounded, tag=None):
+            codes = held(name + "_w", [P, 512], U32, tag)
             scales = held(name + "_s", [P, 512], U8)
             nc.vector.quantize_mx(out=codes[:].bitcast(FP8X4), scales=scales[:], in_=rounded[:])
             return codes, scales
@@ -202,6 +201,7 @@ def tile_list_chest_cough_features_kernel(
 
         y_rows = [held("y_rows%d" % n, [P, S], F32) for n in range(N // P)]
 
+        wavy = [held("wavy0", [P, PACK, HALF], F32, tag="w3_raw1"), held("wavy1", [P, PACK, HALF], F32)]
         waves = {}
 
         def sine(h, t):
@@ -214,7 +214,7 @@ def tile_list_chest_cough_features_kernel(
                     rhs=v_w[a][h][:].bitcast(FP8X4), rhs_scale=v_scale(a, h * HALF, HALF),
                     start=(a == 0), stop=(a == PASSES - 1),
                 )
-            wave = ring.tile([P, HALF], F32, name="wave", bufs=4)
+            wave = ring.tile([P, HALF], F32, name="wave", bufs=8)
             nc.scalar.activation(wave[:], z2[:], ACT.Sin, scale=0.5)
             waves[h, t] = wave
 
@@ -222,7 +222,7 @@ def tile_list_chest_cough_features_kernel(
             wave = waves[h, t]
             nc.scalar.activation(wave[:], wave[:], ACT.Square, scale=root[:, t : t + 1])
             nc.vector.scalar_tensor_tensor(
-                mix[h][:, t, :], wave[:], abs_gain[:, t : t + 1], mix[h][:, t, :], ALU.subtract, ALU.mult
+                wavy[h][:, t, :], wave[:], abs_gain[:, t : t + 1], mix[h][:, t, :], ALU.subtract, ALU.mult
             )
 
         h_round = [held("h_round%d" % h, [P, PACK * HALF], BF16) for h in range(HALVES)]
@@ -242,7 +242,7 @@ def tile_list_chest_cough_features_kernel(
             nc.vector.tensor_tensor(
                 h_round[h][:, PACK * c * CHUNK : PACK * (c + 1) * CHUNK].rearrange("p (c i t) -> p c t i", i=PACK, t=PACK),
                 z3[:].rearrange("p (t c i) -> p c t i", t=PACK, i=PACK),
-                mix[h][:, :, cols].rearrange("p t (c i) -> p c t i", i=PACK),
+                wavy[h][:, :, cols].rearrange("p t (c i) -> p c t i", i=PACK),
                 ALU.add,
             )
 
@@ -272,8 +272,11 @@ def tile_list_chest_cough_features_kernel(
             reading(1, c)
         features(1, (0, 1, 2, 3))
 
+        v2_w = held("v2_w", [P, PAIRS], U32, tag="h_round1")
         nc.vector.tensor_copy(v2_w[:], tab2_w[:].indirect(idx2[:]))
-        w5_codes, w5_scales = quantise("w5", w5_round)
+        w5_codes, w5_scales = quantise("w5", w5_round, tag="wavy1")
+        picked = [held("picked%d" % n, [P, PAIRS], F32) for n in range(N // P)]
+        nc.vector.tensor_copy(picked[0][:], y_rows[0][:].indirect(pair[:]))
         for n in range(N // P):
             b = bank(4 + n)
             nc.tensor.matmul_mx(
@@ -282,8 +285,8 @@ def tile_list_chest_cough_features_kernel(
                 rhs=v2_w[:].bitcast(FP8X4), rhs_scale=v2_s[:],
                 start=True, stop=True,
             )
-            picked = ring.tile([P, PAIRS], F32, name="picked")
-            nc.vector.tensor_copy(picked[:], y_rows[n][:].indirect(pair[:]))
+            if n + 1 < N // P:
+                nc.vector.tensor_copy(picked[n + 1][:], y_rows[n + 1][:].indirect(pair[:]))
             result = ring.tile([P, PAIRS], F32, name="result", bufs=4)
-            nc.vector.tensor_tensor(result[:], b[:], picked[:], ALU.max)
+            nc.vector.tensor_tensor(result[:], b[:], picked[n][:], ALU.max)
             nc.sync.dma_start(out[n * P : (n + 1) * P, :], result[:])

@@ -185,8 +185,8 @@ def tile_list_chest_cough_features_kernel(
                 )
             else:
                 nc.scalar.copy(
-                    rounded[:].rearrange("p (c i j) -> p c j i", i=PACK, j=PACK),
-                    raw[:].rearrange("p j (c i) -> p c j i", i=PACK),
+                    rounded[:].rearrange("p (c i j) -> p c j i", i=2, j=PACK),
+                    raw[:].rearrange("p j (c i) -> p c j i", i=2),
                 )
             return rounded
 
@@ -240,9 +240,9 @@ def tile_list_chest_cough_features_kernel(
                         start=(a == 0), stop=(a == PASSES - 1),
                     )
             nc.vector.tensor_tensor(
-                h_round[h][:, PACK * c * CHUNK : PACK * (c + 1) * CHUNK].rearrange("p (c i t) -> p c t i", i=PACK, t=PACK),
-                z3[:].rearrange("p (t c i) -> p c t i", t=PACK, i=PACK),
-                wavy[h][:, :, cols].rearrange("p t (c i) -> p c t i", i=PACK),
+                h_round[h][:, PACK * c * CHUNK : PACK * (c + 1) * CHUNK].rearrange("p (c i t) -> p c t i", i=2, t=PACK),
+                z3[:].rearrange("p (t c i) -> p c t i", t=PACK, i=2),
+                wavy[h][:, :, cols].rearrange("p t (c i) -> p c t i", i=2),
                 ALU.add,
             )
 
@@ -275,8 +275,7 @@ def tile_list_chest_cough_features_kernel(
         v2_w = held("v2_w", [P, PAIRS], U32, tag="h_round1")
         nc.vector.tensor_copy(v2_w[:], tab2_w[:].indirect(idx2[:]))
         w5_codes, w5_scales = quantise("w5", w5_round, tag="wavy1")
-        picked = [held("picked%d" % n, [P, PAIRS], F32) for n in range(N // P)]
-        nc.vector.tensor_copy(picked[0][:], y_rows[0][:].indirect(pair[:]))
+        coughs = []
         for n in range(N // P):
             b = bank(4 + n)
             nc.tensor.matmul_mx(
@@ -285,8 +284,21 @@ def tile_list_chest_cough_features_kernel(
                 rhs=v2_w[:].bitcast(FP8X4), rhs_scale=v2_s[:],
                 start=True, stop=True,
             )
-            if n + 1 < N // P:
-                nc.vector.tensor_copy(picked[n + 1][:], y_rows[n + 1][:].indirect(pair[:]))
-            result = ring.tile([P, PAIRS], F32, name="result", bufs=4)
-            nc.vector.tensor_tensor(result[:], b[:], picked[n][:], ALU.max)
-            nc.sync.dma_start(out[n * P : (n + 1) * P, :], result[:])
+            coughs.append(b)
+        last = N // P - 1
+        pieces = [(n, 0, PAIRS) for n in range(last)] + [(last, 0, PAIRS // 2), (last, PAIRS // 2, PAIRS)]
+
+        def pick(i):
+            n, c0, c1 = pieces[i]
+            picked = held("picked%d" % i, [P, c1 - c0], F32)
+            nc.vector.tensor_copy(picked[:], y_rows[n][:].indirect(pair[:, c0 // 16 : c1 // 16]))
+            return picked
+
+        ahead = pick(0)
+        for i, (n, c0, c1) in enumerate(pieces):
+            picked = ahead
+            if i + 1 < len(pieces):
+                ahead = pick(i + 1)
+            result = held("result%d" % i, [P, c1 - c0], F32)
+            nc.vector.tensor_tensor(result[:], coughs[n][:, c0:c1], picked[:], ALU.max)
+            nc.sync.dma_start(out[n * P : (n + 1) * P, c0:c1], result[:])

@@ -67,12 +67,10 @@ def tile_list_chest_cough_features_kernel(
         w3_raw = [held("w3_raw%d" % a, [P, PACK, H], F32) for a in range(PASSES)]
         w5_raw = held("w5_raw", [P, PACK, N], F32)
 
-        nc.gpsimd.memset(w1_raw_s[:].bitcast(I32), 0)
         nc.vector.memset(tab_s[32:64, :].bitcast(I32), 0)
         nc.vector.memset(tab_s[64:P, :].bitcast(I32), 0)
-
-        for plane in (v_s, tab2_s, v2_s, w4_s):
-            nc.vector.memset(plane[:].bitcast(I32), 0)
+        for plane in (w1_raw_s, v_s, tab2_s):
+            nc.gpsimd.memset(plane[:].bitcast(I32), 0)
 
         def load_words(dst, src, c0, c1):
             flat = src.rearrange("p n t -> p (n t)")
@@ -84,28 +82,30 @@ def tile_list_chest_cough_features_kernel(
 
         nc.sync.dma_start(idx[:], offs)
         nc.scalar.dma_start(tab_s[0:32, :].bitcast(I32), tab_scales.bitcast(I32).rearrange("a q c -> q a c"))
-        nc.scalar.dma_start(
-            w1_raw[:].bitcast(I32).rearrange("p (a c) -> p a c", a=PASSES),
-            w1_words.bitcast(I32).rearrange("a p c -> p a c"),
-        )
         for q in range(QUADS):
-            nc.gpsimd.dma_start(
+            nc.scalar.dma_start(
                 w1_raw_s[32 * q : 32 * q + 4, :].bitcast(I32).rearrange("r (a c) -> r a c", a=PASSES),
                 w1_scales.bitcast(I32)[:, 4 * q : 4 * q + 4, :].rearrange("a r c -> r a c"),
             )
+        nc.sync.dma_start(
+            w1_raw[:].bitcast(I32).rearrange("p (a c) -> p a c", a=PASSES),
+            w1_words.bitcast(I32).rearrange("a p c -> p a c"),
+        )
         nc.gpsimd.dma_start(gains[:], gain.rearrange("(p t) -> p t", t=PACK))
         nc.gpsimd.dma_start(bias[:], b1.rearrange("(p t) -> p t", t=PACK))
         nc.gpsimd.dma_start(tab2_s[0:P:8, :].bitcast(I32), tab2_scales[0].bitcast(I32))
+        for plane in (v2_s, w4_s):
+            nc.gpsimd.memset(plane[:].bitcast(I32), 0)
         load_words(tab_w[0], tab_words[0], 0, T // 2)
         load_words(tab_w[0], tab_words[0], T // 2, T)
-        nc.sync.dma_start(idx2[:], offs2)
         load_words(tab_w[1], tab_words[1], 0, T // 2)
+        nc.sync.dma_start(idx2[:], offs2)
+        nc.sync.dma_start(pair[:], pos1)
         load_words(tab_w[1], tab_words[1], T // 2, T)
         load_weight(w2_raw[0], w2, 0)
         load_weight(w2_raw[1], w2, 1)
         load_weight(w3_raw[0], w3, 0)
         load_weight(w3_raw[1], w3, 1)
-        nc.sync.dma_start(pair[:], pos1)
         load_words(w4_w, w4_words[0], 0, N)
         load_weight(w5_raw, w5, 0)
         load_words(tab2_w, tab2_words[0], 0, T2)

@@ -228,7 +228,7 @@ def tile_list_chest_cough_features_kernel(
         h_round = [held("h_round%d" % h, [P, PACK * HALF], BF16) for h in range(HALVES)]
 
         def reading(h, c):
-            z3 = bank((CHUNKS * h + c) % 3)
+            z3 = bank(c)
             cols = slice(c * CHUNK, (c + 1) * CHUNK)
             for t in range(PACK):
                 for a in range(PASSES):
@@ -266,7 +266,7 @@ def tile_list_chest_cough_features_kernel(
             if h == 1:
                 reading(0, t)
             ripple(h, t)
-        features(0, (3, 4, 5, 6))
+        features(0, (4, 5, 6, 7))
         w5_round = quantised("w5", w5_raw, False)
         for c in range(CHUNKS):
             reading(1, c)
@@ -286,7 +286,7 @@ def tile_list_chest_cough_features_kernel(
             )
             coughs.append(b)
         last = N // P - 1
-        pieces = [(n, 0, PAIRS) for n in range(last)] + [(last, 0, PAIRS // 2), (last, PAIRS // 2, PAIRS)]
+        pieces = [(n, 0, PAIRS) for n in range(last)] + [(last, 0, PAIRS - 128), (last, PAIRS - 128, PAIRS)]
 
         def pick(i):
             n, c0, c1 = pieces[i]

from contextlib import ExitStack

import concourse.mybir as mybir

K, T, S, H, N, K2, T2, PAIRS = 1024, 4096, 1024, 512, 512, 512, 2048, 512
FLOPS = 2 * (3 * K * H * S + H * N * S + K2 * N * PAIRS)

F32 = mybir.dt.float32
BF16 = mybir.dt.bfloat16
I32 = mybir.dt.int32
U32 = mybir.dt.uint32
U16 = mybir.dt.uint16
U8 = mybir.dt.uint8
FP8X4 = mybir.dt.float8_e4m3fn_x4
FP4X4 = mybir.dt.float4_e2m1fn_x4
ACT = mybir.ActivationFunctionType
ALU = mybir.AluOpType

P = 128
PACK = 4
K_PASS = P * PACK
PASSES = K // K_PASS
HALF = 512
HALVES = S // HALF
CHUNK = 128
CHUNKS = HALF // CHUNK
QUADS = 4


def tile_list_chest_cough_features_kernel(
    tc, tab_words, tab_scales, offs, tab2_words, tab2_scales, offs2, pos1,
    w1_words, w1_scales, b1, w2, gain, w3, w4_words, w4_scales, w5, out,
):
    nc = tc.nc
    with ExitStack() as ctx:
        keep = ctx.enter_context(tc.tile_pool(name="keep", bufs=1))
        ring = ctx.enter_context(tc.tile_pool(name="ring", bufs=2))
        psum = ctx.enter_context(tc.psum_pool(name="psum", bufs=1))

        def held(name, shape, dtype, tag=None):
            return keep.tile(shape, dtype, name=name, tag=tag or name, align_bytes=64)

        def bank(i):
            return psum.tile([P, 512], F32, name="bank%d" % i, tag="bank%d" % i)

        idx = held("idx", [P, S // 16], U16)
        idx2 = held("idx2", [P, PAIRS // 16], U16)
        pair = held("pair", [P, PAIRS // 16], U16)
        tab_w = [held("tab_w%d" % a, [P, T], U32) for a in range(PASSES)]
        tab_s = held("tab_s", [P, T], U8)
        tab2_w = held("tab2_w", [P, T2], U32)
        tab2_s = held("tab2_s", [P, T2], U8)
        v_w = [[held("v_w%d_%d" % (a, h), [P, HALF], U32) for h in range(HALVES)] for a in range(PASSES)]
        v_rows = held("v_rows", [P, S], U8)
        v_s = held("v_s", [P, PASSES * S], U8)
        v2_rows = held("v2_rows", [P, PAIRS], U8)
        v2_s = held("v2_s", [P, PAIRS], U8)
        w1_raw = held("w1_raw", [P, PASSES * 2 * H], U8)
        w1_raw_s = held("w1_raw_s", [P, PASSES * H], U8)
        w1_w = held("w1_w", [P, PASSES * 2 * H], U8)
        w1_s = held("w1_s", [P, PASSES * H], U8)
        w4_w = held("w4_w", [P, N], U32)
        w4_s = held("w4_s", [P, N], U8)
        bias = held("bias", [P, PACK], F32)
        gains = held("gains", [P, PACK], F32)
        w2_raw = [held("w2_raw%d" % a, [P, PACK, H], F32) for a in range(PASSES)]
        w3_raw = [held("w3_raw%d" % a, [P, PACK, H], F32) for a in range(PASSES)]
        w5_raw = held("w5_raw", [P, PACK, N], F32)

        nc.vector.memset(tab_s[32:64, :].bitcast(I32), 0)
        nc.vector.memset(tab_s[64:P, :].bitcast(I32), 0)
        for plane in (w1_raw_s, v_s, tab2_s):
            nc.gpsimd.memset(plane[:].bitcast(I32), 0)

        def load_words(dst, src, c0, c1):
            flat = src.rearrange("p n t -> p (n t)")
            nc.sync.dma_start(dst[:, c0:c1].bitcast(I32), flat[:, PACK * c0 : PACK * c1].bitcast(I32))

        def load_weight(dst, src, a):
            rows = src[a * K_PASS : (a + 1) * K_PASS, :]
            nc.sync.dma_start(dst[:], rows.rearrange("(p j) c -> p j c", j=PACK))

        nc.sync.dma_start(idx[:], offs)
        nc.scalar.dma_start(tab_s[0:32, :].bitcast(I32), tab_scales.bitcast(I32).rearrange("a q c -> q a c"))
        for q in range(QUADS):
            nc.scalar.dma_start(
                w1_raw_s[32 * q : 32 * q + 4, :].bitcast(I32).rearrange("r (a c) -> r a c", a=PASSES),
                w1_scales.bitcast(I32)[:, 4 * q : 4 * q + 4, :].rearrange("a r c -> r a c"),
            )
        nc.sync.dma_start(
            w1_raw[:].bitcast(I32).rearrange("p (a c) -> p a c", a=PASSES),
            w1_words.bitcast(I32).rearrange("a p c -> p a c"),
        )
        nc.gpsimd.dma_start(gains[:], gain.rearrange("(p t) -> p t", t=PACK))
        nc.gpsimd.dma_start(bias[:], b1.rearrange("(p t) -> p t", t=PACK))
        nc.gpsimd.dma_start(tab2_s[0:P:8, :].bitcast(I32), tab2_scales[0].bitcast(I32))
        for plane in (v2_s, w4_s):
            nc.gpsimd.memset(plane[:].bitcast(I32), 0)
        load_words(tab_w[0], tab_words[0], 0, T // 2)
        load_words(tab_w[0], tab_words[0], T // 2, T)
        load_words(tab_w[1], tab_words[1], 0, T // 2)
        nc.sync.dma_start(idx2[:], offs2)
        nc.sync.dma_start(pair[:], pos1)
        load_words(tab_w[1], tab_words[1], T // 2, T)
        load_weight(w2_raw[0], w2, 0)
        load_weight(w2_raw[1], w2, 1)
        load_weight(w3_raw[0], w3, 0)
        load_weight(w3_raw[1], w3, 1)
        load_words(w4_w, w4_words[0], 0, N)
        load_weight(w5_raw, w5, 0)
        load_words(tab2_w, tab2_words[0], 0, T2)
        for q in range(QUADS):
            nc.sync.dma_start(w4_s[32 * q : 32 * q + 4, :].bitcast(I32), w4_scales[0].bitcast(I32)[4 * q : 4 * q + 4, :])

        nc.vector.tensor_copy(v_rows[:], tab_s[:].indirect(idx[:]))
        for q in range(QUADS):
            nc.scalar.dma_start(
                v_s[32 * q : 32 * q + 4, :].bitcast(I32).rearrange("r (a c) -> r a c", a=PASSES),
                v_rows[8 * q : 8 * q + 8, :].bitcast(I32),
            )

        def gather_words(a, h):
            cols = slice(h * HALF // 16, (h + 1) * HALF // 16)
            nc.vector.tensor_copy(v_w[a][h][:], tab_w[a][:].indirect(idx[:, cols]))


        nc.scalar.copy(
            w1_w[:].bitcast(U16).rearrange("p (a t m) -> p a t m", a=PASSES, t=PACK),
            w1_raw[:].bitcast(U16).rearrange("p (a m t) -> p a t m", a=PASSES, t=PACK),
        )
        nc.vector.tensor_copy(
            w1_s[:].rearrange("p (a t m) -> p a t m", a=PASSES, t=PACK),
            w1_raw_s[:].rearrange("p (a m t) -> p a t m", a=PASSES, t=PACK),
        )

        for h in range(HALVES):
            gather_words(0, h)
        nc.vector.tensor_copy(v2_rows[:], tab2_s[:].indirect(idx2[:]))
        for q in range(QUADS):
            nc.sync.dma_start(v2_s[32 * q : 32 * q + 4, :].bitcast(I32), v2_rows[32 * q : 32 * q + 32 : 8, :].bitcast(I32))

        two_abs = held("two_abs", [P, PACK], F32)
        abs_gain = held("abs_gain", [P, PACK], F32)
        flip = held("flip", [P, PACK], F32)
        flip_bias = held("flip_bias", [P, PACK], F32)
        halves = held("halves", [P, PACK], F32)
        root = held("root", [P, PACK], F32)
        nc.scalar.activation(two_abs[:], gains[:], ACT.Abs, scale=2.0)
        nc.scalar.activation(abs_gain[:], gains[:], ACT.Abs)
        nc.scalar.activation(flip[:], gains[:], ACT.Sign, scale=-1.0)
        nc.gpsimd.memset(halves[:], 0.5)
        nc.gpsimd.tensor_tensor(root[:], two_abs[:], halves[:], ALU.pow)
        nc.gpsimd.tensor_tensor(flip_bias[:], bias[:], flip[:], ALU.mult)

        for h in range(HALVES):
            gather_words(1, h)

        def v_scale(a, c0, width):
            return v_s[:, a * S + c0 : a * S + c0 + width]

        mix = [held("mix%d" % h, [P, PACK, HALF], F32) for h in range(HALVES)]
        z1 = [[bank(PACK * h + t) for t in range(PACK)] for h in range(HALVES)]
        for h in range(HALVES):
            for a in range(PASSES):
                for t in range(PACK):
                    c = a * H + t * P
                    nc.tensor.matmul_mx(
                        z1[h][t][:],
                        lhsT=w1_w[:, 2 * c : 2 * (c + P)].bitcast(FP4X4), lhsT_scale=w1_s[:, c : c + P],
                        rhs=v_w[a][h][:].bitcast(FP8X4), rhs_scale=v_scale(a, h * HALF, HALF),
                        start=(a == 0), stop=(a == PASSES - 1),
                    )
        for h in range(HALVES):
            for t in range(PACK):
                nc.scalar.activation(
                    mix[h][:, t, :], z1[h][t][:], ACT.Tanh, bias=flip_bias[:, t : t + 1], scale=flip[:, t : t + 1]
                )

        def quantised(name, raw, dealt):
            rounded = ring.tile([P, PACK * 512], BF16, name="rounded", align_bytes=64)
            if dealt:
                nc.vector.tensor_copy(
                    rounded[:].rearrange("p (t m j) -> p m t j", t=PACK, j=PACK),
                    raw[:].rearrange("p j (m t) -> p m t j", t=PACK),
                )
            else:
                nc.scalar.copy(
                    rounded[:].rearrange("p (c i j) -> p c j i", i=2, j=PACK),
                    raw[:].rearrange("p j (c i) -> p c j i", i=2),
                )
            return rounded

        def quantise(name, rounded, tag=None):
            codes = held(name + "_w", [P, 512], U32, tag)
            scales = held(name + "_s", [P, 512], U8)
            nc.vector.quantize_mx(out=codes[:].bitcast(FP8X4), scales=scales[:], in_=rounded[:])
            return codes, scales

        w2_q = [quantise("w2_%d" % a, quantised("w2", w2_raw[a], True)) for a in range(PASSES)]
        w3_q = [quantise("w3_%d" % a, quantised("w3", w3_raw[a], True)) for a in range(PASSES)]

        y_rows = [held("y_rows%d" % n, [P, S], F32) for n in range(N // P)]

        wavy = [held("wavy0", [P, PACK, HALF], F32, tag="w3_raw1"), held("wavy1", [P, PACK, HALF], F32)]
        waves = {}

        def sine(h, t):
            z2 = bank(PACK * h + t)
            for a in range(PASSES):
                codes, scales = w2_q[a]
                nc.tensor.matmul_mx(
                    z2[:],
                    lhsT=codes[:, t * P : (t + 1) * P].bitcast(FP8X4), lhsT_scale=scales[:, t * P : (t + 1) * P],
                    rhs=v_w[a][h][:].bitcast(FP8X4), rhs_scale=v_scale(a, h * HALF, HALF),
                    start=(a == 0), stop=(a == PASSES - 1),
                )
            wave = ring.tile([P, HALF], F32, name="wave", bufs=8)
            nc.scalar.activation(wave[:], z2[:], ACT.Sin, scale=0.5)
            waves[h, t] = wave

        def ripple(h, t):
            wave = waves[h, t]
            nc.scalar.activation(wave[:], wave[:], ACT.Square, scale=root[:, t : t + 1])
            nc.vector.scalar_tensor_tensor(
                wavy[h][:, t, :], wave[:], abs_gain[:, t : t + 1], mix[h][:, t, :], ALU.subtract, ALU.mult
            )

        h_round = [held("h_round%d" % h, [P, PACK * HALF], BF16) for h in range(HALVES)]

        def reading(h, c):
            z3 = bank(c)
            cols = slice(c * CHUNK, (c + 1) * CHUNK)
            for t in range(PACK):
                for a in range(PASSES):
                    codes, scales = w3_q[a]
                    nc.tensor.matmul_mx(
                        z3[:, t * CHUNK : (t + 1) * CHUNK],
                        lhsT=codes[:, t * P : (t + 1) * P].bitcast(FP8X4), lhsT_scale=scales[:, t * P : (t + 1) * P],
                        rhs=v_w[a][h][:, cols].bitcast(FP8X4), rhs_scale=v_scale(a, h * HALF + c * CHUNK, CHUNK),
                        start=(a == 0), stop=(a == PASSES - 1),
                    )
            nc.vector.tensor_tensor(
                h_round[h][:, PACK * c * CHUNK : PACK * (c + 1) * CHUNK].rearrange("p (c i t) -> p c t i", i=2, t=PACK),
                z3[:].rearrange("p (t c i) -> p c t i", t=PACK, i=2),
                wavy[h][:, :, cols].rearrange("p t (c i) -> p c t i", i=2),
                ALU.add,
            )

        def features(h, banks):
            codes, scales = quantise("h_%d" % h, h_round[h])
            for n in range(N // P):
                y = bank(banks[n])
                nc.tensor.matmul_mx(
                    y[:],
                    lhsT=w4_w[:, n * P : (n + 1) * P].bitcast(FP8X4), lhsT_scale=w4_s[:, n * P : (n + 1) * P],
                    rhs=codes[:].bitcast(FP8X4), rhs_scale=scales[:],
                    start=True, stop=True,
                )
                nc.scalar.copy(y_rows[n][:, h * HALF : (h + 1) * HALF], y[:])

        steps = [(h, t) for h in range(HALVES) for t in range(PACK)]
        sine(*steps[0])
        for i, (h, t) in enumerate(steps):
            if i + 1 < len(steps):
                sine(*steps[i + 1])
            if h == 1:
                reading(0, t)
            ripple(h, t)
        features(0, (4, 5, 6, 7))
        w5_round = quantised("w5", w5_raw, False)
        for c in range(CHUNKS):
            reading(1, c)
        features(1, (0, 1, 2, 3))

        v2_w = held("v2_w", [P, PAIRS], U32, tag="h_round1")
        nc.vector.tensor_copy(v2_w[:], tab2_w[:].indirect(idx2[:]))
        w5_codes, w5_scales = quantise("w5", w5_round, tag="wavy1")
        coughs = []
        for n in range(N // P):
            b = bank(4 + n)
            nc.tensor.matmul_mx(
                b[:],
                lhsT=w5_codes[:, n * P : (n + 1) * P].bitcast(FP8X4), lhsT_scale=w5_scales[:, n * P : (n + 1) * P],
                rhs=v2_w[:].bitcast(FP8X4), rhs_scale=v2_s[:],
                start=True, stop=True,
            )
            coughs.append(b)
        last = N // P - 1
        pieces = [(n, 0, PAIRS) for n in range(last)] + [(last, 0, PAIRS - 128), (last, PAIRS - 128, PAIRS)]

        def pick(i):
            n, c0, c1 = pieces[i]
            picked = held("picked%d" % i, [P, c1 - c0], F32)
            nc.vector.tensor_copy(picked[:], y_rows[n][:].indirect(pair[:, c0 // 16 : c1 // 16]))
            return picked

        ahead = pick(0)
        for i, (n, c0, c1) in enumerate(pieces):
            picked = ahead
            if i + 1 < len(pieces):
                ahead = pick(i + 1)
            result = held("result%d" % i, [P, c1 - c0], F32)
            nc.vector.tensor_tensor(result[:], coughs[n][:, c0:c1], picked[:], ALU.max)
            nc.sync.dma_start(out[n * P : (n + 1) * P, c0:c1], result[:])
